import numpy as np
import ml_dtypes


def mxq(x, axis, fmt="e4m3"):
    dtype, down = {"e4m3": (ml_dtypes.float8_e4m3fn, 7), "e5m2": (ml_dtypes.float8_e5m2, 14)}[fmt]
    v = np.moveaxis(np.asarray(x, np.float32).astype(ml_dtypes.bfloat16).astype(np.float64), axis, -1)
    blocks = v.reshape(v.shape[:-1] + (-1, 32))
    amax = np.abs(blocks).max(-1, keepdims=True)
    byte = np.maximum(np.where(amax > 0, np.frexp(amax)[1] - 1 + 127, 0) - down, 1)
    scale = np.exp2(byte - 127.0)
    codes = (blocks / scale).astype(np.float32).astype(dtype).astype(np.float64)
    return np.moveaxis((codes * scale).reshape(v.shape), -1, axis)


WIDE = False


def mx_kscale(k):
    if not WIDE:
        return np.ones(k)
    levels = np.array([10, -10, 5, -5, 0])
    if k % 512:
        return np.exp2(np.random.permutation(np.resize(levels, k // 32))).repeat(32)
    a = np.empty((k // 512, 16))
    for p in range(k // 512):
        a[p, :8] = np.random.permutation(np.resize(levels, 8))
        for g in range(8):
            far = levels[np.abs(levels - a[p, g]) >= 10]
            a[p, g + 8] = far[np.random.randint(len(far))]
    return np.exp2(a.ravel()).repeat(32)


BF16 = ml_dtypes.bfloat16


def bf(x):
    return np.asarray(x, np.float32).astype(BF16)


def f64(x):
    return np.asarray(x).astype(np.float64)

def planes(Y):
    n, m = Y.shape
    b = f64(bf(Y)).reshape(n // 32, 32, m)
    amax = np.abs(b).max(1)
    byte = np.clip(np.where(amax > 0, np.frexp(amax)[1] - 1 + 127 - 7, 1), 1, 254)
    codes = (b * np.exp2(127.0 - byte)[:, None, :]).reshape(n, m).astype(np.float32).astype(ml_dtypes.float8_e4m3fn).view(np.uint8)
    words = codes.reshape(n // 512, 128, 4, m).transpose(0, 1, 3, 2)
    return np.ascontiguousarray(words), np.ascontiguousarray(byte.astype(np.uint8).reshape(n // 512, 16, m))


J, N, D, V, A = 3, 1024, 1024, 1024, 512


def softmax(v):
    e = np.exp(v - v.max(axis=-1, keepdims=True))
    return e / e.sum(axis=-1, keepdims=True)


def setup_inputs():
    s = np.stack([mx_kscale(D) for _ in range(J)])
    u = mx_kscale(N)
    return {"hs": bf(np.random.standard_normal((J, N, D)) * s[:, None, :]),
            "ws": bf(np.random.standard_normal((J, D, V)) / np.sqrt(D) / s[:, :, None]),
            "a": bf(np.random.standard_normal((N, A)) * u[:, None]),
            "wt": bf(np.random.standard_normal(N) * (V / (32.0 * np.sqrt(N))) / u)}


def expert_logits(hs, ws):
    return mxq(f64(hs), 2, "e4m3") @ mxq(f64(ws), 1, "e4m3")


def proxy_tuned_teacher(z):
    return softmax(z[0] + z[1] - z[2])


def core(hs, ws, a, wt):
    z = expert_logits(hs, ws)
    pt = proxy_tuned_teacher(z)
    p0 = softmax(z[0])
    dz = 32.0 * f64(wt)[:, None] * (p0 - pt)
    return mxq(f64(a), 0, "e4m3").T @ mxq(dz, 0, "e4m3")


def reference(hs, ws, a, wt):
    R_out = core(hs, ws, a, wt)
    words, scales = planes(R_out)
    return R_out, words, scales

@@ -1,0 +1,454 @@
+from contextlib import ExitStack
+
+import concourse.mybir as mybir
+from concourse.masks import make_identity
+
+J, N, D, V, A = 3, 1024, 1024, 1024, 512
+FLOPS = 2 * J * N * D * V + 2 * A * N * V
+
+F32 = mybir.dt.float32
+BF16 = mybir.dt.bfloat16
+U32 = mybir.dt.uint32
+I32 = mybir.dt.int32
+U8 = mybir.dt.uint8
+FP8X4 = mybir.dt.float8_e4m3fn_x4
+ALU = mybir.AluOpType
+ACTF = mybir.ActivationFunctionType
+AX = mybir.AxisListType.X
+
+P = 128
+HALF = 512
+
+
+def tile_proxytunedteacherzeroinitsideadaptergrad_x1_kernel(tc, hs, ws, a, wt, out_0, out_1, out_2):
+    nc = tc.nc
+    with ExitStack() as ctx:
+        keep = ctx.enter_context(tc.tile_pool(name="keep", bufs=1))
+        rawp = ctx.enter_context(tc.tile_pool(name="rawp", bufs=5))
+        grpp = ctx.enter_context(tc.tile_pool(name="grpp", bufs=4))
+        hgp = ctx.enter_context(tc.tile_pool(name="hgp", bufs=4))
+        esp = ctx.enter_context(tc.tile_pool(name="esp", bufs=4))
+        dzp = ctx.enter_context(tc.tile_pool(name="dzp", bufs=1))
+        small = ctx.enter_context(tc.tile_pool(name="small", bufs=6))
+        psum = ctx.enter_context(tc.psum_pool(name="psum", bufs=1))
+
+        ident = keep.tile([P, P], F32, name="ident")
+        make_identity(nc, ident[:])
+        warm = keep.tile([P, 1], F32, name="warm")
+        nc.vector.memset(warm[:], 0.0)
+        nc.scalar.activation(out=warm[:], in_=warm[:], func=ACTF.Exp)
+
+        raw = {}
+
+        def load_hs(j, g, t0, t1):
+            tl = rawp.tile([P, t1 - t0, D], BF16, name="raw" if t1 - t0 == 4 else "raw4", bufs=5 if t1 - t0 == 4 else 6, align_bytes=64)
+            for t in range(t0, t1):
+                raw[("h", j, 4 * g + t)] = tl[:, t - t0, :]
+            view = hs[j, 512 * g : 512 * (g + 1), :].rearrange("(p t) k -> p t k", t=4)
+            nc.sync.dma_start(out=tl[:], in_=view[:, t0:t1, :])
+
+        def load_ws(j, g, lo=0, hi=V):
+            n = hi - lo
+            tl = rawp.tile([P, 4, n], BF16, name="raw" if n == V else "raw4", bufs=5 if n == V else 6, align_bytes=64)
+            for h in range(lo // HALF, hi // HALF):
+                raw[("w", j, g, h)] = tl[:, :, HALF * h - lo : HALF * (h + 1) - lo]
+            view = ws[j, 512 * g : 512 * (g + 1), :].rearrange("(p r) v -> p r v", r=4)
+            nc.sync.dma_start(out=tl[:], in_=view[:, :, lo:hi])
+
+        def load_a():
+            raw["a"] = rawp.tile([P, 2, 4, A], BF16, name="raw", align_bytes=64)
+            for g in range(2):
+                view = a[512 * g : 512 * (g + 1), :].rearrange("(p r) c -> p r c", r=4)
+                nc.sync.dma_start(out=raw["a"][:, g, :, :], in_=view)
+
+        wtt = {}
+
+        def load_wt():
+            for g in range(2):
+                wtt[g] = keep.tile([P, 4], BF16, name="wtt_%d" % g)
+                nc.sync.dma_start(out=wtt[g][:], in_=wt[512 * g : 512 * (g + 1)].rearrange("(p t) -> p t", t=4))
+
+        wc = {}
+        wsc = {}
+        grp = {}
+
+        def w_copy(j, g, h, on_act):
+            if (j, g) not in wc:
+                wc[(j, g)] = keep.tile([P, V], U32, name="wc_%d_%d" % (j, g), align_bytes=64)
+                wsc[(j, g)] = keep.tile([P, V], U8, name="wsc_%d_%d" % (j, g), align_bytes=64)
+            t = grpp.tile([P, HALF, 4], BF16, name="grp", align_bytes=64)
+            grp[(j, g, h)] = t
+            src = raw[("w", j, g, h)].rearrange("p r v -> p v r")
+            if j == 2:
+                if on_act:
+                    nc.scalar.activation(out=t[:], in_=src, func=ACTF.Copy, scale=-1.0)
+                else:
+                    nc.vector.tensor_scalar(out=t[:], in0=src, scalar1=-1.0, scalar2=None, op0=ALU.mult)
+            else:
+                if on_act:
+                    nc.scalar.copy(out=t[:], in_=src)
+                else:
+                    nc.vector.tensor_copy(out=t[:], in_=src)
+
+        def w_quant(j, g, h):
+            cols = slice(HALF * h, HALF * (h + 1))
+            nc.vector.quantize_mx(
+                out=wc[(j, g)][:, cols].bitcast(FP8X4),
+                scales=wsc[(j, g)][:, cols],
+                in_=grp[(j, g, h)][:].rearrange("p v r -> p (v r)"),
+            )
+
+        hc = {}
+        hsc = {}
+        trs = {}
+        hgs = {}
+
+        def h_trans(j, i):
+            tr = psum.tile([P, 4, P], F32, name="bank", bufs=8)
+            trs[(j, i)] = tr
+            words = raw[("h", j, i)].bitcast(F32)
+            for q in range(2):
+                for u in range(2):
+                    nc.tensor.transpose(tr[:, 2 * q + u, :], words[:, 256 * q + u : 256 * (q + 1) : 2], ident[:])
+
+        def h_copy(j, i, on_act):
+            hg = hgp.tile([P, D], BF16, name="hg", align_bytes=64)
+            hgs[(j, i)] = hg
+            dst = hg[:].bitcast(F32).rearrange("p (q r u) -> p q r u", q=2, u=2)
+            src = trs[(j, i)][:].rearrange("p (q u) r -> p q r u", q=2)
+            if on_act:
+                nc.scalar.copy(out=dst, in_=src)
+            else:
+                nc.vector.tensor_copy(out=dst, in_=src)
+
+        def h_quant(j, i):
+            hc[(j, i)] = keep.tile([P, 256], U32, name="hc_%d_%d" % (j, i), align_bytes=64)
+            hsc[(j, i)] = keep.tile([P, 256], U8, name="hsc_%d_%d" % (j, i), align_bytes=64)
+            nc.vector.quantize_mx(out=hc[(j, i)][:].bitcast(FP8X4), scales=hsc[(j, i)][:], in_=hgs[(j, i)][:])
+
+        def z_mm(models, i):
+            z = [psum.tile([P, HALF], F32, name="bank", bufs=8) for h in range(2)]
+            passes = [(j, q) for j in models for q in range(2)]
+            for h in range(2):
+                cols = slice(HALF * h, HALF * (h + 1))
+                for n, (j, q) in enumerate(passes):
+                    rows = slice(P * q, P * (q + 1))
+                    nc.tensor.matmul_mx(
+                        out=z[h][:],
+                        lhsT=hc[(j, i)][:, rows].bitcast(FP8X4),
+                        lhsT_scale=hsc[(j, i)][:, rows],
+                        rhs=wc[(j, q)][:, cols].bitcast(FP8X4),
+                        rhs_scale=wsc[(j, q)][:, cols],
+                        start=(n == 0),
+                        stop=(n == len(passes) - 1),
+                    )
+            return z
+
+        def z_max(z, h, mx):
+            nc.vector.tensor_reduce(out=mx[:, h : h + 1], in_=z[h][:], axis=AX, op=ALU.max)
+
+        def z_neg(mx):
+            nm = small.tile([P, 1], F32, name="nm")
+            nc.vector.tensor_scalar(out=nm[:], in0=mx[:, 0:1], scalar1=mx[:, 1:2], scalar2=-1.0, op0=ALU.max, op1=ALU.mult)
+            return nm
+
+        def z_exp(z, nm, e, s):
+            for h in range(2):
+                nc.scalar.activation(
+                    out=e[:, HALF * h : HALF * (h + 1)], in_=z[h][:], func=ACTF.Exp, bias=nm[:], scale=1.0,
+                    accum_out=s[:, h : h + 1],
+                )
+
+        e0 = {}
+        s0 = {}
+        c0 = {}
+        es = {}
+        ncs = {}
+
+        def c0_all(g):
+            s = keep.tile([P, 4], F32, name="s0s_%d" % g)
+            nc.vector.tensor_reduce(out=s[:], in_=s0[g][:], axis=AX, op=ALU.add)
+            r = keep.tile([P, 4], F32, name="r0_%d" % g)
+            nc.vector.reciprocal(out=r[:], in_=s[:])
+            c0[g] = keep.tile([P, 4], F32, name="c0_%d" % g)
+            nc.vector.scalar_tensor_tensor(out=c0[g][:], in0=r[:], scalar=32.0, in1=wtt[g][:], op0=ALU.mult, op1=ALU.mult)
+
+        sts = {}
+
+        def ncs_a(i):
+            st = small.tile([P, 1], F32, name="st")
+            nc.vector.tensor_tensor(out=st[:], in0=ss[i][:, 0:1], in1=ss[i][:, 1:2], op=ALU.add)
+            sts[i] = st
+
+        def ncs_b(i):
+            rt = small.tile([P, 1], F32, name="rt")
+            nc.vector.reciprocal(out=rt[:], in_=sts[i][:])
+            sts[i] = rt
+
+        def ncs_c(i):
+            g, t = divmod(i, 4)
+            ncs[i] = small.tile([P, 1], F32, name="nct")
+            nc.vector.scalar_tensor_tensor(
+                out=ncs[i][:], in0=sts[i][:], scalar=-32.0, in1=wtt[g][:, t : t + 1], op0=ALU.mult, op1=ALU.mult
+            )
+
+        dzb = {}
+        dc = {}
+        dsc = {}
+        dg = {}
+
+        def e0_scale(i):
+            g, t = divmod(i, 4)
+            nc.scalar.activation(out=e0[i][:], in_=e0[i][:], func=ACTF.Copy, scale=c0[g][:, t : t + 1])
+
+        def dz_comb(i, lo, hi):
+            g, t = divmod(i, 4)
+            if g not in dzb:
+                dzb[g] = dzp.tile([P, 4, V], BF16, name="dzb_%d" % g)
+            nc.vector.scalar_tensor_tensor(
+                out=dzb[g][:, t, lo:hi], in0=es[i][:, lo:hi], scalar=ncs[i][:], in1=e0[i][:, lo:hi], op0=ALU.mult, op1=ALU.add
+            )
+
+        def dz_il(g, h, lo, hi, on_act):
+            if (g, h) not in dg:
+                dg[(g, h)] = grpp.tile([P, HALF, 4], BF16, name="grp", align_bytes=64)
+            src = dzb[g][:, :, HALF * h + lo : HALF * h + hi].rearrange("p t v -> p v t")
+            if on_act:
+                nc.scalar.copy(out=dg[(g, h)][:, lo:hi, :], in_=src)
+            else:
+                nc.vector.tensor_copy(out=dg[(g, h)][:, lo:hi, :], in_=src)
+
+        def dz_quant(g, h, lo, hi):
+            if (g, h) not in dc:
+                dc[(g, h)] = keep.tile([P, HALF], U32, name="dc_%d_%d" % (g, h), align_bytes=64)
+                dsc[(g, h)] = keep.tile([P, HALF], U8, name="dsc_%d_%d" % (g, h), align_bytes=64)
+            nc.vector.quantize_mx(
+                out=dc[(g, h)][:, lo:hi].bitcast(FP8X4), scales=dsc[(g, h)][:, lo:hi],
+                in_=dg[(g, h)][:, lo:hi, :].rearrange("p v t -> p (v t)"),
+            )
+
+        ac = {}
+        asc = {}
+        ag = {}
+
+        def a_copy(g, on_act):
+            t = grpp.tile([P, HALF, 4], BF16, name="grp", align_bytes=64)
+            ag[g] = t
+            dst = t[:].rearrange("p (t m) r -> p t m r", t=4)
+            src = raw["a"][:, g, :, :].rearrange("p r (m t) -> p t m r", t=4)
+            if on_act:
+                nc.scalar.copy(out=dst, in_=src)
+            else:
+                nc.vector.tensor_copy(out=dst, in_=src)
+
+        def a_quant(g):
+            ac[g] = keep.tile([P, A], U32, name="ac_%d" % g, align_bytes=64)
+            asc[g] = keep.tile([P, A], U8, name="asc_%d" % g, align_bytes=64)
+            nc.vector.quantize_mx(
+                out=ac[g][:].bitcast(FP8X4), scales=asc[g][:], in_=ag[g][:].rearrange("p c r -> p (c r)")
+            )
+
+        load_hs(0, 0, 0, 2)
+        load_ws(0, 0)
+        load_ws(0, 1)
+        load_hs(0, 0, 2, 4)
+        load_wt()
+        load_hs(0, 1, 0, 4)
+        load_ws(1, 0)
+        load_hs(1, 0, 0, 4)
+        load_ws(1, 1)
+        load_hs(2, 0, 0, 4)
+        load_ws(2, 0)
+        load_ws(2, 1)
+        load_hs(1, 1, 0, 4)
+        load_hs(2, 1, 0, 4)
+        load_a()
+
+        h_trans(0, 0)
+        h_trans(0, 1)
+        h_copy(0, 0, True)
+        h_copy(0, 1, True)
+        w_copy(0, 0, 0, False)
+        w_copy(0, 0, 1, True)
+        h_quant(0, 0)
+        h_quant(0, 1)
+        w_quant(0, 0, 0)
+        w_copy(0, 1, 0, False)
+        w_quant(0, 0, 1)
+        w_quant(0, 1, 0)
+        w_copy(0, 1, 1, False)
+        h_trans(0, 2)
+        h_trans(0, 3)
+        h_copy(0, 2, True)
+        h_copy(0, 3, True)
+        h_quant(0, 2)
+        w_quant(0, 1, 1)
+        h_quant(0, 3)
+
+        h_list = [(0, 4), (0, 5), (0, 6), (0, 7)] + [(j, i) for i in range(8) for j in (1, 2)]
+        w_list = [(1, 0, 0), (1, 0, 1), (1, 1, 0), (1, 1, 1), (2, 0, 0), (2, 0, 1), (2, 1, 0), (2, 1, 1)]
+        w_act = {(1, 0, 1), (1, 1, 1), (2, 0, 1)}
+        zs = {}
+        nms = {}
+        for g in range(2):
+            s0[g] = keep.tile([P, 4, 2], F32, name="s0_%d" % g)
+        for i in range(8):
+            e0[i] = keep.tile([P, V], F32, name="e0_%d" % i)
+
+        wq = []
+        for i in range(8):
+            hh = h_list[2 * i : 2 * i + 2]
+            wi = w_list[i]
+            for x in hh:
+                h_trans(*x)
+            zs[i] = z_mm([0], i)
+            for x in hh:
+                h_copy(*x, on_act=True)
+            w_copy(*wi, on_act=wi in w_act)
+            if wq:
+                w_quant(*wq.pop())
+            mx = small.tile([P, 2], F32, name="mx")
+            z_max(zs[i], 0, mx)
+            h_quant(*hh[0])
+            z_max(zs[i], 1, mx)
+            h_quant(*hh[1])
+            nms[i] = z_neg(mx)
+            z_exp(zs[i], nms[i], e0[i], s0[i // 4][:, i % 4, :])
+            wq.append(wi)
+            if i == 4:
+                c0_all(0)
+
+        zt = {}
+        nmt = {}
+        ss = {}
+        for i in range(8):
+            hh = h_list[16 + 2 * i : 18 + 2 * i]
+            zt[i] = z_mm([0, 1, 2], i) if i else None
+            for x in hh:
+                h_trans(*x)
+                h_copy(*x, on_act=True)
+            if i == 0:
+                w_quant(*wq.pop())
+                zt[i] = z_mm([0, 1, 2], i)
+            for x in hh:
+                h_quant(*x)
+            if i == 1:
+                c0_all(1)
+            mx = small.tile([P, 2], F32, name="mx")
+            z_max(zt[i], 0, mx)
+            if i > 0:
+                ncs_a(i - 1)
+            if i in (1, 2):
+                a_quant(i - 1)
+            if i == 6:
+                dz_quant(0, 0, 0, 512)
+                dz_quant(0, 1, 0, 512)
+            z_max(zt[i], 1, mx)
+            if i > 0:
+                ncs_b(i - 1)
+            if i > 1:
+                dz_comb(i - 2, 0, V)
+            nmt[i] = z_neg(mx)
+            if i > 0:
+                ncs_c(i - 1)
+            if i < 2:
+                a_copy(i, False)
+            e0_scale(i)
+            if i == 5:
+                dz_il(0, 0, 0, 512, True)
+                dz_il(0, 1, 0, 512, False)
+            es[i] = esp.tile([P, V], F32, name="es")
+            ss[i] = small.tile([P, 2], F32, name="sst")
+            z_exp(zt[i], nmt[i], es[i], ss[i])
+        ob = {}
+
+        def o_alloc(h):
+            for t in range(4):
+                ob[(h, t)] = psum.tile([P, HALF], F32, name="bank", bufs=8)
+
+        def o_mm(h, t, g):
+            rows = slice(P * t, P * (t + 1))
+            nc.tensor.matmul_mx(
+                out=ob[(h, t)][:], lhsT=ac[g][:, rows].bitcast(FP8X4), lhsT_scale=asc[g][:, rows],
+                rhs=dc[(g, h)][:].bitcast(FP8X4), rhs_scale=dsc[(g, h)][:], start=(g == 0), stop=(g == 1),
+            )
+
+        res = {}
+        oc = keep.tile([P, V], U32, name="oc", align_bytes=64)
+        osc = keep.tile([P, V], U8, name="osc", align_bytes=64)
+        og = {}
+
+        def o_copy(h, t, on_act):
+            if h not in res:
+                res[h] = rawp.tile([P, 4, HALF], F32, name="raw", align_bytes=64)
+            if on_act:
+                nc.scalar.copy(out=res[h][:, t, :], in_=ob[(h, t)][:])
+            else:
+                nc.vector.tensor_copy(out=res[h][:, t, :], in_=ob[(h, t)][:])
+
+        def o_store(h):
+            cols = slice(HALF * h, HALF * (h + 1))
+            nc.sync.dma_start(out=out_0[:, cols].rearrange("(p t) m -> p t m", t=4), in_=res[h][:])
+
+        def o_il(h, lo, hi, on_act):
+            if h not in og:
+                og[h] = grpp.tile([P, HALF, 4], BF16, name="grp", align_bytes=64)
+            src = res[h][:, :, lo:hi].rearrange("p t m -> p m t")
+            if on_act:
+                nc.scalar.copy(out=og[h][:, lo:hi, :], in_=src)
+            else:
+                nc.vector.tensor_copy(out=og[h][:, lo:hi, :], in_=src)
+
+        def o_quant(h, lo, hi):
+            cols = slice(HALF * h + lo, HALF * h + hi)
+            nc.vector.quantize_mx(
+                out=oc[:, cols].bitcast(FP8X4), scales=osc[:, cols], in_=og[h][:, lo:hi, :].rearrange("p m t -> p (m t)")
+            )
+
+        def planes_store(h):
+            cols = slice(HALF * h, HALF * (h + 1))
+            nc.sync.dma_start(
+                out=out_1[0, :, cols, :].rearrange("p m t -> p (m t)").bitcast(I32), in_=oc[:, cols].bitcast(I32)
+            )
+            for q in range(4):
+                nc.sync.dma_start(
+                    out=out_2[0, 4 * q : 4 * q + 4, cols].bitcast(I32), in_=osc[32 * q : 32 * q + 4, cols].bitcast(I32)
+                )
+
+        for h in range(2):
+            o_alloc(h)
+            for t in range(4):
+                o_mm(h, t, 0)
+        ncs_a(7)
+        dz_comb(6, 0, 512)
+        ncs_b(7)
+        dz_comb(6, 512, 1024)
+        ncs_c(7)
+        for k in (0, 1, 3):
+            dz_comb(7, 256 * k, 256 * (k + 1))
+        dz_il(1, 0, 0, 256, False)
+        dz_il(1, 0, 256, 512, False)
+        dz_quant(1, 0, 0, 256)
+        dz_comb(7, 512, 768)
+        dz_quant(1, 0, 256, 512)
+        dz_il(1, 1, 256, 512, True)
+        dz_il(1, 1, 0, 256, False)
+        dz_quant(1, 1, 256, 512)
+        dz_quant(1, 1, 0, 256)
+        for h in range(2):
+            for t in range(4):
+                o_mm(h, t, 1)
+        for t in range(4):
+            o_copy(0, t, t != 3)
+        o_store(0)
+        o_il(0, 0, 512, False)
+        for t in range(4):
+            o_copy(1, t, t < 2)
+        o_quant(0, 0, 512)
+        planes_store(0)
+        o_store(1)
+        o_il(1, 0, 256, False)
+        o_il(1, 256, 512, True)
+        o_quant(1, 0, 256)
+        o_quant(1, 256, 512)
+        planes_store(1)

@@ -78,17 +78,18 @@ def tile_proxytunedteacherzeroinitsideadaptergrad_x1_kernel(tc, hs, ws, a, wt, o
                 wsc[(j, g)] = keep.tile([P, V], U8, name="wsc_%d_%d" % (j, g), align_bytes=64)
             t = grpp.tile([P, HALF, 4], BF16, name="grp", align_bytes=64)
             grp[(j, g, h)] = t
-            src = raw[("w", j, g, h)].rearrange("p r v -> p v r")
+            src = raw[("w", j, g, h)].rearrange("p r (c i) -> p c r i", i=4)
+            dst = t[:].rearrange("p (c i) r -> p c r i", i=4)
             if j == 2:
                 if on_act:
-                    nc.scalar.activation(out=t[:], in_=src, func=ACTF.Copy, scale=-1.0)
+                    nc.scalar.activation(out=dst, in_=src, func=ACTF.Copy, scale=-1.0)
                 else:
-                    nc.vector.tensor_scalar(out=t[:], in0=src, scalar1=-1.0, scalar2=None, op0=ALU.mult)
+                    nc.vector.tensor_scalar(out=dst, in0=src, scalar1=-1.0, scalar2=None, op0=ALU.mult)
             else:
                 if on_act:
-                    nc.scalar.copy(out=t[:], in_=src)
+                    nc.scalar.copy(out=dst, in_=src)
                 else:
-                    nc.vector.tensor_copy(out=t[:], in_=src)
+                    nc.vector.tensor_copy(out=dst, in_=src)
 
         def w_quant(j, g, h):
             cols = slice(HALF * h, HALF * (h + 1))
@@ -212,11 +213,12 @@ def tile_proxytunedteacherzeroinitsideadaptergrad_x1_kernel(tc, hs, ws, a, wt, o
         def dz_il(g, h, lo, hi, on_act):
             if (g, h) not in dg:
                 dg[(g, h)] = grpp.tile([P, HALF, 4], BF16, name="grp", align_bytes=64)
-            src = dzb[g][:, :, HALF * h + lo : HALF * h + hi].rearrange("p t v -> p v t")
+            src = dzb[g][:, :, HALF * h + lo : HALF * h + hi].rearrange("p t (c i) -> p c t i", i=4)
+            dst = dg[(g, h)][:, lo:hi, :].rearrange("p (c i) t -> p c t i", i=4)
             if on_act:
-                nc.scalar.copy(out=dg[(g, h)][:, lo:hi, :], in_=src)
+                nc.scalar.copy(out=dst, in_=src)
             else:
-                nc.vector.tensor_copy(out=dg[(g, h)][:, lo:hi, :], in_=src)
+                nc.vector.tensor_copy(out=dst, in_=src)
 
         def dz_quant(g, h, lo, hi):
             if (g, h) not in dc:

from contextlib import ExitStack

import concourse.mybir as mybir
from concourse.masks import make_identity

J, N, D, V, A = 3, 1024, 1024, 1024, 512
FLOPS = 2 * J * N * D * V + 2 * A * N * V

F32 = mybir.dt.float32
BF16 = mybir.dt.bfloat16
U32 = mybir.dt.uint32
I32 = mybir.dt.int32
U8 = mybir.dt.uint8
FP8X4 = mybir.dt.float8_e4m3fn_x4
ALU = mybir.AluOpType
ACTF = mybir.ActivationFunctionType
AX = mybir.AxisListType.X

P = 128
HALF = 512


def tile_proxytunedteacherzeroinitsideadaptergrad_x1_kernel(tc, hs, ws, a, wt, out_0, out_1, out_2):
    nc = tc.nc
    with ExitStack() as ctx:
        keep = ctx.enter_context(tc.tile_pool(name="keep", bufs=1))
        rawp = ctx.enter_context(tc.tile_pool(name="rawp", bufs=5))
        grpp = ctx.enter_context(tc.tile_pool(name="grpp", bufs=4))
        hgp = ctx.enter_context(tc.tile_pool(name="hgp", bufs=4))
        esp = ctx.enter_context(tc.tile_pool(name="esp", bufs=4))
        dzp = ctx.enter_context(tc.tile_pool(name="dzp", bufs=1))
        small = ctx.enter_context(tc.tile_pool(name="small", bufs=6))
        psum = ctx.enter_context(tc.psum_pool(name="psum", bufs=1))

        ident = keep.tile([P, P], F32, name="ident")
        make_identity(nc, ident[:])
        warm = keep.tile([P, 1], F32, name="warm")
        nc.vector.memset(warm[:], 0.0)
        nc.scalar.activation(out=warm[:], in_=warm[:], func=ACTF.Exp)

        raw = {}

        def load_hs(j, g, t0, t1):
            tl = rawp.tile([P, t1 - t0, D], BF16, name="raw" if t1 - t0 == 4 else "raw4", bufs=5 if t1 - t0 == 4 else 6, align_bytes=64)
            for t in range(t0, t1):
                raw[("h", j, 4 * g + t)] = tl[:, t - t0, :]
            view = hs[j, 512 * g : 512 * (g + 1), :].rearrange("(p t) k -> p t k", t=4)
            nc.sync.dma_start(out=tl[:], in_=view[:, t0:t1, :])

        def load_ws(j, g, lo=0, hi=V):
            n = hi - lo
            tl = rawp.tile([P, 4, n], BF16, name="raw" if n == V else "raw4", bufs=5 if n == V else 6, align_bytes=64)
            for h in range(lo // HALF, hi // HALF):
                raw[("w", j, g, h)] = tl[:, :, HALF * h - lo : HALF * (h + 1) - lo]
            view = ws[j, 512 * g : 512 * (g + 1), :].rearrange("(p r) v -> p r v", r=4)
            nc.sync.dma_start(out=tl[:], in_=view[:, :, lo:hi])

        def load_a():
            raw["a"] = rawp.tile([P, 2, 4, A], BF16, name="raw", align_bytes=64)
            for g in range(2):
                view = a[512 * g : 512 * (g + 1), :].rearrange("(p r) c -> p r c", r=4)
                nc.sync.dma_start(out=raw["a"][:, g, :, :], in_=view)

        wtt = {}

        def load_wt():
            for g in range(2):
                wtt[g] = keep.tile([P, 4], BF16, name="wtt_%d" % g)
                nc.sync.dma_start(out=wtt[g][:], in_=wt[512 * g : 512 * (g + 1)].rearrange("(p t) -> p t", t=4))

        wc = {}
        wsc = {}
        grp = {}

        def w_copy(j, g, h, on_act):
            if (j, g) not in wc:
                wc[(j, g)] = keep.tile([P, V], U32, name="wc_%d_%d" % (j, g), align_bytes=64)
                wsc[(j, g)] = keep.tile([P, V], U8, name="wsc_%d_%d" % (j, g), align_bytes=64)
            t = grpp.tile([P, HALF, 4], BF16, name="grp", align_bytes=64)
            grp[(j, g, h)] = t
            src = raw[("w", j, g, h)].rearrange("p r (c i) -> p c r i", i=4)
            dst = t[:].rearrange("p (c i) r -> p c r i", i=4)
            if j == 2:
                if on_act:
                    nc.scalar.activation(out=dst, in_=src, func=ACTF.Copy, scale=-1.0)
                else:
                    nc.vector.tensor_scalar(out=dst, in0=src, scalar1=-1.0, scalar2=None, op0=ALU.mult)
            else:
                if on_act:
                    nc.scalar.copy(out=dst, in_=src)
                else:
                    nc.vector.tensor_copy(out=dst, in_=src)

        def w_quant(j, g, h):
            cols = slice(HALF * h, HALF * (h + 1))
            nc.vector.quantize_mx(
                out=wc[(j, g)][:, cols].bitcast(FP8X4),
                scales=wsc[(j, g)][:, cols],
                in_=grp[(j, g, h)][:].rearrange("p v r -> p (v r)"),
            )

        hc = {}
        hsc = {}
        trs = {}
        hgs = {}

        def h_trans(j, i):
            tr = psum.tile([P, 4, P], F32, name="bank", bufs=8)
            trs[(j, i)] = tr
            words = raw[("h", j, i)].bitcast(F32)
            for q in range(2):
                for u in range(2):
                    nc.tensor.transpose(tr[:, 2 * q + u, :], words[:, 256 * q + u : 256 * (q + 1) : 2], ident[:])

        def h_copy(j, i, on_act):
            hg = hgp.tile([P, D], BF16, name="hg", align_bytes=64)
            hgs[(j, i)] = hg
            dst = hg[:].bitcast(F32).rearrange("p (q r u) -> p q r u", q=2, u=2)
            src = trs[(j, i)][:].rearrange("p (q u) r -> p q r u", q=2)
            if on_act:
                nc.scalar.copy(out=dst, in_=src)
            else:
                nc.vector.tensor_copy(out=dst, in_=src)

        def h_quant(j, i):
            hc[(j, i)] = keep.tile([P, 256], U32, name="hc_%d_%d" % (j, i), align_bytes=64)
            hsc[(j, i)] = keep.tile([P, 256], U8, name="hsc_%d_%d" % (j, i), align_bytes=64)
            nc.vector.quantize_mx(out=hc[(j, i)][:].bitcast(FP8X4), scales=hsc[(j, i)][:], in_=hgs[(j, i)][:])

        def z_mm(models, i):
            z = [psum.tile([P, HALF], F32, name="bank", bufs=8) for h in range(2)]
            passes = [(j, q) for j in models for q in range(2)]
            for h in range(2):
                cols = slice(HALF * h, HALF * (h + 1))
                for n, (j, q) in enumerate(passes):
                    rows = slice(P * q, P * (q + 1))
                    nc.tensor.matmul_mx(
                        out=z[h][:],
                        lhsT=hc[(j, i)][:, rows].bitcast(FP8X4),
                        lhsT_scale=hsc[(j, i)][:, rows],
                        rhs=wc[(j, q)][:, cols].bitcast(FP8X4),
                        rhs_scale=wsc[(j, q)][:, cols],
                        start=(n == 0),
                        stop=(n == len(passes) - 1),
                    )
            return z

        def z_max(z, h, mx):
            nc.vector.tensor_reduce(out=mx[:, h : h + 1], in_=z[h][:], axis=AX, op=ALU.max)

        def z_neg(mx):
            nm = small.tile([P, 1], F32, name="nm")
            nc.vector.tensor_scalar(out=nm[:], in0=mx[:, 0:1], scalar1=mx[:, 1:2], scalar2=-1.0, op0=ALU.max, op1=ALU.mult)
            return nm

        def z_exp(z, nm, e, s):
            for h in range(2):
                nc.scalar.activation(
                    out=e[:, HALF * h : HALF * (h + 1)], in_=z[h][:], func=ACTF.Exp, bias=nm[:], scale=1.0,
                    accum_out=s[:, h : h + 1],
                )

        e0 = {}
        s0 = {}
        c0 = {}
        es = {}
        ncs = {}

        def c0_all(g):
            s = keep.tile([P, 4], F32, name="s0s_%d" % g)
            nc.vector.tensor_reduce(out=s[:], in_=s0[g][:], axis=AX, op=ALU.add)
            r = keep.tile([P, 4], F32, name="r0_%d" % g)
            nc.vector.reciprocal(out=r[:], in_=s[:])
            c0[g] = keep.tile([P, 4], F32, name="c0_%d" % g)
            nc.vector.scalar_tensor_tensor(out=c0[g][:], in0=r[:], scalar=32.0, in1=wtt[g][:], op0=ALU.mult, op1=ALU.mult)

        sts = {}

        def ncs_a(i):
            st = small.tile([P, 1], F32, name="st")
            nc.vector.tensor_tensor(out=st[:], in0=ss[i][:, 0:1], in1=ss[i][:, 1:2], op=ALU.add)
            sts[i] = st

        def ncs_b(i):
            rt = small.tile([P, 1], F32, name="rt")
            nc.vector.reciprocal(out=rt[:], in_=sts[i][:])
            sts[i] = rt

        def ncs_c(i):
            g, t = divmod(i, 4)
            ncs[i] = small.tile([P, 1], F32, name="nct")
            nc.vector.scalar_tensor_tensor(
                out=ncs[i][:], in0=sts[i][:], scalar=-32.0, in1=wtt[g][:, t : t + 1], op0=ALU.mult, op1=ALU.mult
            )

        dzb = {}
        dc = {}
        dsc = {}
        dg = {}

        def e0_scale(i):
            g, t = divmod(i, 4)
            nc.scalar.activation(out=e0[i][:], in_=e0[i][:], func=ACTF.Copy, scale=c0[g][:, t : t + 1])

        def dz_comb(i, lo, hi):
            g, t = divmod(i, 4)
            if g not in dzb:
                dzb[g] = dzp.tile([P, 4, V], BF16, name="dzb_%d" % g)
            nc.vector.scalar_tensor_tensor(
                out=dzb[g][:, t, lo:hi], in0=es[i][:, lo:hi], scalar=ncs[i][:], in1=e0[i][:, lo:hi], op0=ALU.mult, op1=ALU.add
            )

        def dz_il(g, h, lo, hi, on_act):
            if (g, h) not in dg:
                dg[(g, h)] = grpp.tile([P, HALF, 4], BF16, name="grp", align_bytes=64)
            src = dzb[g][:, :, HALF * h + lo : HALF * h + hi].rearrange("p t (c i) -> p c t i", i=4)
            dst = dg[(g, h)][:, lo:hi, :].rearrange("p (c i) t -> p c t i", i=4)
            if on_act:
                nc.scalar.copy(out=dst, in_=src)
            else:
                nc.vector.tensor_copy(out=dst, in_=src)

        def dz_quant(g, h, lo, hi):
            if (g, h) not in dc:
                dc[(g, h)] = keep.tile([P, HALF], U32, name="dc_%d_%d" % (g, h), align_bytes=64)
                dsc[(g, h)] = keep.tile([P, HALF], U8, name="dsc_%d_%d" % (g, h), align_bytes=64)
            nc.vector.quantize_mx(
                out=dc[(g, h)][:, lo:hi].bitcast(FP8X4), scales=dsc[(g, h)][:, lo:hi],
                in_=dg[(g, h)][:, lo:hi, :].rearrange("p v t -> p (v t)"),
            )

        ac = {}
        asc = {}
        ag = {}

        def a_copy(g, on_act):
            t = grpp.tile([P, HALF, 4], BF16, name="grp", align_bytes=64)
            ag[g] = t
            dst = t[:].rearrange("p (t m) r -> p t m r", t=4)
            src = raw["a"][:, g, :, :].rearrange("p r (m t) -> p t m r", t=4)
            if on_act:
                nc.scalar.copy(out=dst, in_=src)
            else:
                nc.vector.tensor_copy(out=dst, in_=src)

        def a_quant(g):
            ac[g] = keep.tile([P, A], U32, name="ac_%d" % g, align_bytes=64)
            asc[g] = keep.tile([P, A], U8, name="asc_%d" % g, align_bytes=64)
            nc.vector.quantize_mx(
                out=ac[g][:].bitcast(FP8X4), scales=asc[g][:], in_=ag[g][:].rearrange("p c r -> p (c r)")
            )

        load_hs(0, 0, 0, 2)
        load_ws(0, 0)
        load_ws(0, 1)
        load_hs(0, 0, 2, 4)
        load_wt()
        load_hs(0, 1, 0, 4)
        load_ws(1, 0)
        load_hs(1, 0, 0, 4)
        load_ws(1, 1)
        load_hs(2, 0, 0, 4)
        load_ws(2, 0)
        load_ws(2, 1)
        load_hs(1, 1, 0, 4)
        load_hs(2, 1, 0, 4)
        load_a()

        h_trans(0, 0)
        h_trans(0, 1)
        h_copy(0, 0, True)
        h_copy(0, 1, True)
        w_copy(0, 0, 0, False)
        w_copy(0, 0, 1, True)
        h_quant(0, 0)
        h_quant(0, 1)
        w_quant(0, 0, 0)
        w_copy(0, 1, 0, False)
        w_quant(0, 0, 1)
        w_quant(0, 1, 0)
        w_copy(0, 1, 1, False)
        h_trans(0, 2)
        h_trans(0, 3)
        h_copy(0, 2, True)
        h_copy(0, 3, True)
        h_quant(0, 2)
        w_quant(0, 1, 1)
        h_quant(0, 3)

        h_list = [(0, 4), (0, 5), (0, 6), (0, 7)] + [(j, i) for i in range(8) for j in (1, 2)]
        w_list = [(1, 0, 0), (1, 0, 1), (1, 1, 0), (1, 1, 1), (2, 0, 0), (2, 0, 1), (2, 1, 0), (2, 1, 1)]
        w_act = {(1, 0, 1), (1, 1, 1), (2, 0, 1)}
        zs = {}
        nms = {}
        for g in range(2):
            s0[g] = keep.tile([P, 4, 2], F32, name="s0_%d" % g)
        for i in range(8):
            e0[i] = keep.tile([P, V], F32, name="e0_%d" % i)

        wq = []
        for i in range(8):
            hh = h_list[2 * i : 2 * i + 2]
            wi = w_list[i]
            for x in hh:
                h_trans(*x)
            zs[i] = z_mm([0], i)
            for x in hh:
                h_copy(*x, on_act=True)
            w_copy(*wi, on_act=wi in w_act)
            if wq:
                w_quant(*wq.pop())
            mx = small.tile([P, 2], F32, name="mx")
            z_max(zs[i], 0, mx)
            h_quant(*hh[0])
            z_max(zs[i], 1, mx)
            h_quant(*hh[1])
            nms[i] = z_neg(mx)
            z_exp(zs[i], nms[i], e0[i], s0[i // 4][:, i % 4, :])
            wq.append(wi)
            if i == 4:
                c0_all(0)

        zt = {}
        nmt = {}
        ss = {}
        for i in range(8):
            hh = h_list[16 + 2 * i : 18 + 2 * i]
            zt[i] = z_mm([0, 1, 2], i) if i else None
            for x in hh:
                h_trans(*x)
                h_copy(*x, on_act=True)
            if i == 0:
                w_quant(*wq.pop())
                zt[i] = z_mm([0, 1, 2], i)
            for x in hh:
                h_quant(*x)
            if i == 1:
                c0_all(1)
            mx = small.tile([P, 2], F32, name="mx")
            z_max(zt[i], 0, mx)
            if i > 0:
                ncs_a(i - 1)
            if i in (1, 2):
                a_quant(i - 1)
            if i == 6:
                dz_quant(0, 0, 0, 512)
                dz_quant(0, 1, 0, 512)
            z_max(zt[i], 1, mx)
            if i > 0:
                ncs_b(i - 1)
            if i > 1:
                dz_comb(i - 2, 0, V)
            nmt[i] = z_neg(mx)
            if i > 0:
                ncs_c(i - 1)
            if i < 2:
                a_copy(i, False)
            e0_scale(i)
            if i == 5:
                dz_il(0, 0, 0, 512, True)
                dz_il(0, 1, 0, 512, False)
            es[i] = esp.tile([P, V], F32, name="es")
            ss[i] = small.tile([P, 2], F32, name="sst")
            z_exp(zt[i], nmt[i], es[i], ss[i])
        ob = {}

        def o_alloc(h):
            for t in range(4):
                ob[(h, t)] = psum.tile([P, HALF], F32, name="bank", bufs=8)

        def o_mm(h, t, g):
            rows = slice(P * t, P * (t + 1))
            nc.tensor.matmul_mx(
                out=ob[(h, t)][:], lhsT=ac[g][:, rows].bitcast(FP8X4), lhsT_scale=asc[g][:, rows],
                rhs=dc[(g, h)][:].bitcast(FP8X4), rhs_scale=dsc[(g, h)][:], start=(g == 0), stop=(g == 1),
            )

        res = {}
        oc = keep.tile([P, V], U32, name="oc", align_bytes=64)
        osc = keep.tile([P, V], U8, name="osc", align_bytes=64)
        og = {}

        def o_copy(h, t, on_act):
            if h not in res:
                res[h] = rawp.tile([P, 4, HALF], F32, name="raw", align_bytes=64)
            if on_act:
                nc.scalar.copy(out=res[h][:, t, :], in_=ob[(h, t)][:])
            else:
                nc.vector.tensor_copy(out=res[h][:, t, :], in_=ob[(h, t)][:])

        def o_store(h):
            cols = slice(HALF * h, HALF * (h + 1))
            nc.sync.dma_start(out=out_0[:, cols].rearrange("(p t) m -> p t m", t=4), in_=res[h][:])

        def o_il(h, lo, hi, on_act):
            if h not in og:
                og[h] = grpp.tile([P, HALF, 4], BF16, name="grp", align_bytes=64)
            src = res[h][:, :, lo:hi].rearrange("p t m -> p m t")
            if on_act:
                nc.scalar.copy(out=og[h][:, lo:hi, :], in_=src)
            else:
                nc.vector.tensor_copy(out=og[h][:, lo:hi, :], in_=src)

        def o_quant(h, lo, hi):
            cols = slice(HALF * h + lo, HALF * h + hi)
            nc.vector.quantize_mx(
                out=oc[:, cols].bitcast(FP8X4), scales=osc[:, cols], in_=og[h][:, lo:hi, :].rearrange("p m t -> p (m t)")
            )

        def planes_store(h):
            cols = slice(HALF * h, HALF * (h + 1))
            nc.sync.dma_start(
                out=out_1[0, :, cols, :].rearrange("p m t -> p (m t)").bitcast(I32), in_=oc[:, cols].bitcast(I32)
            )
            for q in range(4):
                nc.sync.dma_start(
                    out=out_2[0, 4 * q : 4 * q + 4, cols].bitcast(I32), in_=osc[32 * q : 32 * q + 4, cols].bitcast(I32)
                )

        for h in range(2):
            o_alloc(h)
            for t in range(4):
                o_mm(h, t, 0)
        ncs_a(7)
        dz_comb(6, 0, 512)
        ncs_b(7)
        dz_comb(6, 512, 1024)
        ncs_c(7)
        for k in (0, 1, 3):
            dz_comb(7, 256 * k, 256 * (k + 1))
        dz_il(1, 0, 0, 256, False)
        dz_il(1, 0, 256, 512, False)
        dz_quant(1, 0, 0, 256)
        dz_comb(7, 512, 768)
        dz_quant(1, 0, 256, 512)
        dz_il(1, 1, 256, 512, True)
        dz_il(1, 1, 0, 256, False)
        dz_quant(1, 1, 256, 512)
        dz_quant(1, 1, 0, 256)
        for h in range(2):
            for t in range(4):
                o_mm(h, t, 1)
        for t in range(4):
            o_copy(0, t, t != 3)
        o_store(0)
        o_il(0, 0, 512, False)
        for t in range(4):
            o_copy(1, t, t < 2)
        o_quant(0, 0, 512)
        planes_store(0)
        o_store(1)
        o_il(1, 0, 256, False)
        o_il(1, 256, 512, True)
        o_quant(1, 0, 256)
        o_quant(1, 256, 512)
        planes_store(1)
